import numpy as np
import ml_dtypes


def mxq(x, axis, fmt="e4m3"):
    dtype, down = {"e4m3": (ml_dtypes.float8_e4m3fn, 7), "e5m2": (ml_dtypes.float8_e5m2, 14)}[fmt]
    v = np.moveaxis(np.asarray(x, np.float32).astype(ml_dtypes.bfloat16).astype(np.float64), axis, -1)
    blocks = v.reshape(v.shape[:-1] + (-1, 32))
    amax = np.abs(blocks).max(-1, keepdims=True)
    byte = np.maximum(np.where(amax > 0, np.frexp(amax)[1] - 1 + 127, 0) - down, 1)
    scale = np.exp2(byte - 127.0)
    codes = (blocks / scale).astype(np.float32).astype(dtype).astype(np.float64)
    return np.moveaxis((codes * scale).reshape(v.shape), -1, axis)


WIDE = False


def mx_kscale(k):
    if not WIDE:
        return np.ones(k)
    levels = np.array([10, -10, 5, -5, 0])
    if k % 512:
        return np.exp2(np.random.permutation(np.resize(levels, k // 32))).repeat(32)
    a = np.empty((k // 512, 16))
    for p in range(k // 512):
        a[p, :8] = np.random.permutation(np.resize(levels, 8))
        for g in range(8):
            far = levels[np.abs(levels - a[p, g]) >= 10]
            a[p, g + 8] = far[np.random.randint(len(far))]
    return np.exp2(a.ravel()).repeat(32)


BF16 = ml_dtypes.bfloat16


def bf(x):
    return np.asarray(x, np.float32).astype(BF16)


def f64(x):
    return np.asarray(x).astype(np.float64)


E2M1 = np.array([0.0, 0.5, 1.0, 1.5, 2.0, 3.0, 4.0, 6.0, -0.0, -0.5, -1.0, -1.5, -2.0, -3.0, -4.0, -6.0])


def pack_weight(w, fmt):
    k, n = w.shape
    w = f64(bf(w)).reshape(k // 32, 32, n)
    amax = np.abs(w).max(1)
    if fmt == "e4m3":
        byte = np.frexp(amax)[1] - 1 + 127 - 7
    else:
        mant, ex = np.frexp(amax / 6.0)
        byte = np.where(mant > 0.5, ex, ex - 1) + 127
    byte = np.clip(np.where(amax > 0, byte, 1), 1, 254)
    scaled = (w * np.exp2(127.0 - byte)[:, None, :]).reshape(k, n).astype(np.float32)
    by_word = np.ascontiguousarray(scaled.reshape(k // 512, 128, 4, n).transpose(0, 1, 3, 2))
    if fmt == "e4m3":
        words = by_word.astype(ml_dtypes.float8_e4m3fn).view(np.uint8)
    else:
        c = by_word.astype(ml_dtypes.float4_e2m1fn).view(np.uint8) & 0xF
        words = c[..., 0::2] | (c[..., 1::2] << 4)
    return np.ascontiguousarray(words), np.ascontiguousarray(byte.astype(np.uint8).reshape(k // 512, 16, n))


def unpack_weight(words, scales, fmt):
    g, p, n, _ = words.shape
    if fmt == "e4m3":
        vals = np.ascontiguousarray(words).view(ml_dtypes.float8_e4m3fn).astype(np.float64)
    else:
        nib = np.empty((g, p, n, 4), np.uint8)
        nib[..., 0::2] = words & 0xF
        nib[..., 1::2] = words >> 4
        vals = E2M1[nib]
    vals = vals * np.repeat(np.exp2(scales.astype(np.float64) - 127.0), 8, axis=1)[..., None]
    return vals.transpose(0, 1, 3, 2).reshape(g * 512, n)
def pack4(w):
    words, scales = pack_weight(w, "e2m1")
    return words.reshape(words.shape[0], 128, -1), scales


def unpack4(words, scales):
    return unpack_weight(words.reshape(words.shape[0], 128, -1, 2), scales, "e2m1")


E, J, N, P, R = 1024, 512, 2048, 1024, 512

LOG_HAZARD_STD = 0.5
AT_RISK_SCALE = 4.0


def setup_inputs():
    s = mx_kscale(P)
    u = mx_kscale(J)
    t = mx_kscale(N)
    beta = np.random.standard_normal((P, R)) * LOG_HAZARD_STD / np.sqrt(P)
    b_words, b_scales = pack4(beta / s[:, None])
    return {"x": bf(np.random.standard_normal((N, P)) * s),
            "b_words": b_words,
            "b_scales": b_scales,
            "z": bf(np.random.standard_normal((N, R)) * t[:, None]),
            "phi": bf(np.random.standard_normal((E, J)) * u),
            "c": bf(np.random.standard_normal((J, N)) * AT_RISK_SCALE / np.sqrt(J * N) / u[:, None] / t)}


def reference(x, b_words, b_scales, z, phi, c):
    eta = mxq(f64(x), 1, "e4m3") @ unpack4(b_words, b_scales)
    v = np.exp(eta) * f64(z)
    a = np.maximum(mxq(f64(phi), 1, "e4m3") @ mxq(f64(c), 0, "e4m3"), 0.0)
    return mxq(a, 1, "e4m3") @ mxq(v, 0, "e4m3")

@@ -1,0 +1,334 @@
+from contextlib import ExitStack
+
+import concourse.mybir as mybir
+from concourse.masks import make_identity
+
+F32 = mybir.dt.float32
+BF16 = mybir.dt.bfloat16
+I32 = mybir.dt.int32
+U32 = mybir.dt.uint32
+U8 = mybir.dt.uint8
+FP8X4 = mybir.dt.float8_e4m3fn_x4
+FP4X4 = mybir.dt.float4_e2m1fn_x4
+ACT = mybir.ActivationFunctionType
+
+E, J, N, PK, R = 1024, 512, 2048, 1024, 512
+FLOPS = 2 * N * PK * R + 2 * E * J * N + 2 * E * N * R
+P = 128
+
+TENSOR_ORDER = (
+    "TX0 TX1 TX2 TX3 H1 H0 TX4 TX5 H2 TP1 TP2 TP0 H4 A2.0 "
+    "H3 A3.0 H5 A5.0 TX6 TX7 TX9 TX8 A1.1 A3.1 A3.2 A0.1 TP3 TX11 "
+    "TX10 H6 A1.2 H7 A1.0 H8 A0.0 A4.0 A3.3 A2.1 TX12 TX15 TX13 TX14 "
+    "A4.1 A2.2 A2.3 A6.3 H10 A4.2 H11 A1.3 H9 A4.3 O2.0 A0.2 H14 H12 "
+    "O0.0 H13 H15 O1.0 O3.0 O1.1 A0.3 O0.1 A7.2 O2.1 A6.1 O3.1 A6.0 A5.1 "
+    "A7.1 O0.2 O1.2 O2.2 A7.3 O3.2 A6.2 O4.0 A5.3 O4.1 A7.0 A5.2 O4.2 O3.3 "
+    "O1.3 O6.0 O2.3 O6.1 O6.2 O6.3 O4.3 O7.0 O5.0 O7.1 O0.3 O7.2 O7.3 O5.1 "
+    "O5.2 O5.3 "
+)
+VECTOR_ORDER = (
+    "EX0 QX0 QX2 IC0 QX4 QC0 QP1 IC1 QP2 IC2 QC1 QP0 QC2 IC3 "
+    "QX6 QX8 QC3 MUL0.1 EP3 QX10 RA1.0 RA3.1 MUL0.0 QA0.1 RA2.1 QP3 QV0.0 MUL1.0 "
+    "RA2.3 EX14 QA2.0 QX14 QX12 QA0.0 MUL1.1 QA3.0 QV1.0 MUL2.0 MUL2.1 QA0.2 QV2.0 QA4.0 "
+    "MUL3.1 MUL3.0 QA0.3 QV3.0 QA6.0 QA7.0 QA5.0 EO7 "
+)
+LOAD_ORDER = "x0 x1 x2 bw bs x4 c0 p1 p2 p0 c1 c2 x6 x8 c3 p3 x10 z0 x14 x12 z2 z1 z3"
+WARM = 18
+
+
+def parse(name):
+    kind = "".join([ch for ch in name if ch in "ABCEHILMOPQRTUVX"])
+    return kind, [int(v) for v in name.replace(kind, "").split(".")]
+
+
+def a_group(b, g):
+    if b < 2:
+        return [(0, g), (1, g)]
+    return [(b, k) for k in range(4)]
+
+
+def needs(name):
+    kind, a = parse(name)
+    if kind in ("TX", "TP", "IC"):
+        return []
+    if kind == "EX":
+        return ["TX%d" % a[0]]
+    if kind == "QX":
+        return ["EX%d" % a[0], "EX%d" % (a[0] + 1)]
+    if kind == "H":
+        return ["QX%d" % (a[0] - a[0] % 2)]
+    if kind == "EXP":
+        return ["H%d" % a[0]]
+    if kind == "MUL":
+        return ["EXP%d" % (4 * a[0] + t) for t in range(4)]
+    if kind == "QV":
+        return ["MUL%d.0" % a[0], "MUL%d.1" % a[0]]
+    if kind == "QC":
+        return ["IC%d" % a[0]]
+    if kind == "EP":
+        return ["TP%d" % a[0]]
+    if kind == "QP":
+        return ["EP%d" % a[0]]
+    if kind == "A":
+        return ["QP%d" % (a[0] // 2), "QC%d" % a[1]]
+    if kind == "RA":
+        return ["A%d.%d" % (a[0], a[1])]
+    if kind == "QA":
+        return ["RA%d.%d" % key for key in a_group(a[0], a[1])]
+    if kind == "O":
+        return ["QA%d.%d" % a_group(a[0], a[1])[0], "QV%d.0" % a[1]]
+    return ["O%d.3" % a[0]]
+
+
+def program():
+    scalar_order = []
+    for name in TENSOR_ORDER.split():
+        kind, a = parse(name)
+        if kind == "O":
+            reader = "EO%d" % a[0] if a[1] == 3 else None
+        else:
+            reader = {"TX": "EX", "TP": "EP", "H": "EXP", "A": "RA"}[kind] + name.replace(kind, "")
+        if reader is not None and reader not in VECTOR_ORDER.split():
+            scalar_order.append(reader)
+    queues = [scalar_order, VECTOR_ORDER.split(), TENSOR_ORDER.split()]
+    heads = [0, 0, 0]
+    emitted = set()
+    free_banks = 8
+    steps = []
+    total = sum(len(q) for q in queues)
+    while_guard = range(total)
+    for turn in while_guard:
+        pick = None
+        for k in range(3):
+            if pick is None and heads[k] < len(queues[k]):
+                name = queues[k][heads[k]]
+                kind, a = parse(name)
+                opens = k == 2 and (kind != "O" or a[1] == 0)
+                if all(d in emitted for d in needs(name)) and (free_banks > 0 or not opens):
+                    pick = k
+        name = queues[pick][heads[pick]]
+        heads[pick] = heads[pick] + 1
+        emitted.add(name)
+        kind, a = parse(name)
+        eng = "SVT"[pick]
+        if pick == 2 and (kind != "O" or a[1] == 0):
+            free_banks -= 1
+        if kind in ("EX", "EP", "EXP", "RA", "EO"):
+            free_banks += 1
+        if kind == "QX":
+            steps.append((kind, [a[0], a[0] + 1]))
+        elif kind == "QA":
+            steps.append((kind, a_group(a[0], a[1])))
+        elif kind == "MUL":
+            steps.append((kind, a[0], a[1], 2))
+        elif kind == "QV":
+            steps.append((kind, a[0], [0, 1], 2))
+        else:
+            steps.append(tuple([kind] + a + [eng]))
+    return steps
+
+
+def tile_cox_risk_sums_s11_kernel(tc, x, b_words, b_scales, z, phi, c, out):
+    nc = tc.nc
+    with ExitStack() as ctx:
+        keep = ctx.enter_context(tc.tile_pool(name="keep", bufs=1))
+        stage = ctx.enter_context(tc.tile_pool(name="stage", bufs=2))
+        psum = ctx.enter_context(tc.psum_pool(name="psum", bufs=1))
+        ctx.enter_context(tc.manual_schedule())
+
+        x_rows = x.rearrange("(g m t) k -> g m (t k)", g=4, t=4)
+        z_rows = z.rearrange("(g m t) r -> g m (t r)", g=4, t=4)
+        c_rows = c.rearrange("(p j) n -> p j n", j=4)
+        phi_rows = phi.rearrange("(p b) j -> p (b j)", b=8)
+        out_rows = out.rearrange("(p b) r -> p b r", b=8)
+
+        ident = keep.tile([P, P], F32, name="ident")
+        make_identity(nc, ident[:])
+        warm = keep.tile([P, 8], F32, name="warm")
+        bs = keep.tile([P, 1024], U8, name="bs", align_bytes=64)
+        nc.vector.memset(bs[:].bitcast(I32), 0)
+        nc.vector.memset(warm[:, 0:4], 0.0)
+        nc.scalar.activation(out=warm[:, 4:5], in_=warm[:, 0:1], func=ACT.Exp)
+        bw = keep.tile([P, 2048], U8, name="bw", align_bytes=64)
+
+        xraw = [keep.tile([P, 2048], BF16, name="x%d" % s, align_bytes=64) for s in range(8)]
+        zraw = [keep.tile([P, 2048], BF16, name="z%d" % g, align_bytes=64) for g in range(4)]
+        craw = [keep.tile([P, 2048], BF16, name="c%d" % g, align_bytes=64) for g in range(4)]
+        praw = [keep.tile([P, 1024], BF16, name="phi%d" % k, align_bytes=64) for k in range(4)]
+        for item in LOAD_ORDER.split():
+            if item == "bw":
+                nc.sync.dma_start(out=bw[:].bitcast(I32).rearrange("p (h n) -> p h n", h=2),
+                                  in_=b_words.bitcast(I32).rearrange("h p n -> p h n"))
+            elif item == "bs":
+                for q in range(4):
+                    nc.sync.dma_start(
+                        out=bs[32 * q:32 * q + 4, :].bitcast(I32).rearrange("r (h n) -> r h n", h=2),
+                        in_=b_scales.bitcast(I32)[:, 4 * q:4 * q + 4, :].rearrange("h r n -> r h n"))
+            else:
+                kind, i = item[0], int(item[1:])
+                if kind == "x":
+                    cnt = 1 if i < 2 else 2
+                    g, t0 = divmod(i, 4)
+                    nc.sync.dma_start(out=xraw[i // 2][:, (i % 2) * 1024:(i % 2 + cnt) * 1024],
+                                      in_=x_rows[g, :, t0 * 1024:(t0 + cnt) * 1024])
+                elif kind == "z":
+                    nc.sync.dma_start(out=zraw[i][:], in_=z_rows[i])
+                elif kind == "c":
+                    nc.sync.dma_start(out=craw[i][:].rearrange("p (j n) -> p j n", j=4), in_=c_rows[:, :, i * 512:(i + 1) * 512])
+                else:
+                    nc.sync.dma_start(out=praw[i][:], in_=phi_rows[:, i * 1024:(i + 1) * 1024])
+
+        free = list(range(8))
+        banks = {}
+        bank_index = {}
+
+        def open_bank(key):
+            index = free[0]
+            free.remove(index)
+            bank_index[key] = index
+            banks[key] = psum.tile([P, 512], F32, name="bank%d" % index, tag="bank%d" % index)
+            return banks[key]
+
+        def close_bank(key):
+            free.append(bank_index[key])
+
+        def copy_out(eng, dst, src):
+            if eng == "S":
+                nc.scalar.copy(out=dst, in_=src)
+            else:
+                nc.vector.tensor_copy(out=dst, in_=src)
+
+        def quantise(name, src, words):
+            codes = keep.tile([P, words], U32, name=name + "_codes", align_bytes=64)
+            scales = keep.tile([P, words], U8, name=name + "_scales", align_bytes=64)
+            nc.vector.quantize_mx(out=codes[:].bitcast(FP8X4), scales=scales[:], in_=src)
+            return codes, scales
+
+        if WARM:
+            ones = keep.tile([P, 512], BF16, name="ones", align_bytes=64)
+            nc.vector.memset(ones[:].bitcast(I32), 0x3F803F80)
+            wcodes, wscales = quantise("warm", ones[:], P)
+            wbank = psum.tile([P, 512], F32, name="bank7", tag="bank7")
+            for i in range(WARM):
+                nc.tensor.matmul_mx(out=wbank[:, (i % 4) * P:(i % 4 + 1) * P], lhsT=wcodes[:].bitcast(FP8X4), lhsT_scale=wscales[:],
+                                    rhs=wcodes[:].bitcast(FP8X4), rhs_scale=wscales[:], start=True, stop=True)
+
+        steps = program()
+        xgroup, agroup = {}, {}
+        for st in steps:
+            if st[0] == "QX":
+                for j, u in enumerate(st[1]):
+                    xgroup[u] = (st[1][0], j, len(st[1]))
+            if st[0] == "QA":
+                for j, key in enumerate(st[1]):
+                    agroup[key] = (st[1][0], j, len(st[1]))
+        xg, xq, ex, vb, cg, cq, pg, pq, ab, aq = {}, {}, {}, {}, {}, {}, {}, {}, {}, {}
+        vcodes = [keep.tile([P, 512], U32, name="vcodes%d" % g, align_bytes=64) for g in range(4)]
+        vscales = [keep.tile([P, 512], U8, name="vscales%d" % g, align_bytes=64) for g in range(4)]
+
+        def transpose4(key, tl, j):
+            bank = open_bank(key)
+            words = tl[:].bitcast(F32)
+            for h in range(2):
+                for u in range(2):
+                    w0 = 512 * j + 256 * h
+                    nc.tensor.transpose(bank[:, (2 * h + u) * P:(2 * h + u + 1) * P],
+                                        words[:, w0 + u:w0 + 256:2], ident[:])
+
+        def evacuate4(eng, key, tl, j):
+            close_bank(key)
+            copy_out(eng, tl[:].bitcast(F32)[:, 512 * j:512 * (j + 1)].rearrange("q (h m u) -> q h m u", h=2, u=2),
+                     banks[key][:].rearrange("q (h u m) -> q h m u", h=2, u=2))
+
+        for st in steps:
+            kind = st[0]
+            if kind == "TX":
+                transpose4(("X", st[1]), xraw[st[1] // 2], st[1] % 2)
+            elif kind == "EX":
+                evacuate4(st[2], ("X", st[1]), xraw[st[1] // 2], st[1] % 2)
+            elif kind == "QX":
+                first = st[1][0]
+                xq[first] = quantise("xq%d" % first, xraw[first // 2][:], 256 * len(st[1]))
+            elif kind == "H":
+                first, j, cnt = xgroup[st[1]]
+                codes, scales = xq[first]
+                bank = open_bank(("H", st[1]))
+                for h in range(2):
+                    cols = slice((2 * j + h) * P, (2 * j + h + 1) * P)
+                    nc.tensor.matmul_mx(out=bank[:], lhsT=codes[:, cols].bitcast(FP8X4), lhsT_scale=scales[:, cols],
+                                        rhs=bw[:, 1024 * h:1024 * (h + 1)].bitcast(FP4X4),
+                                        rhs_scale=bs[:, 512 * h:512 * (h + 1)], start=(h == 0), stop=(h == 1))
+            elif kind == "EXP":
+                g, t = divmod(st[1], 4)
+                if g not in ex:
+                    ex[g] = stage.tile([P, 2048], F32, name="ex", tag="ex", bufs=4, align_bytes=64)
+                nc.scalar.activation(out=ex[g][:, 512 * t:512 * (t + 1)], in_=banks[("H", st[1])][:], func=ACT.Exp)
+                close_bank(("H", st[1]))
+            elif kind == "MUL":
+                g, h, nh = st[1], st[2], st[3]
+                vb[g] = craw[g]
+                cs = slice(h * (128 // nh), (h + 1) * (128 // nh))
+                nc.vector.tensor_tensor(
+                    out=vb[g][:].rearrange("p (c i t) -> p c t i", i=4, t=4)[:, cs],
+                    in0=ex[g][:].rearrange("p (t c i) -> p c t i", i=4, t=4)[:, cs],
+                    in1=zraw[g][:].rearrange("p (t c i) -> p c t i", i=4, t=4)[:, cs],
+                    op=mybir.AluOpType.mult)
+            elif kind == "QV":
+                g, hs, nh = st[1], st[2], st[3]
+                w = 512 // nh
+                lo, hi = hs[0] * w, (hs[-1] + 1) * w
+                nc.vector.quantize_mx(out=vcodes[g][:, lo:hi].bitcast(FP8X4), scales=vscales[g][:, lo:hi],
+                                      in_=vb[g][:, 4 * lo:4 * hi])
+            elif kind == "IC":
+                g = st[1]
+                cg[g] = stage.tile([P, 2048], BF16, name="cg", tag="cg", bufs=2, align_bytes=64)
+                copy_out(st[2], cg[g][:].rearrange("p (t a b j) -> p a t b j", t=4, b=2, j=4),
+                         craw[g][:].rearrange("p (j a b t) -> p a t b j", j=4, b=2, t=4))
+            elif kind == "QC":
+                cq[st[1]] = quantise("cq%d" % st[1], cg[st[1]][:], 512)
+            elif kind == "TP":
+                transpose4(("P", st[1]), praw[st[1]], 0)
+            elif kind == "EP":
+                evacuate4(st[2], ("P", st[1]), praw[st[1]], 0)
+            elif kind == "QP":
+                pq[st[1]] = quantise("pq%d" % st[1], praw[st[1]][:], 256)
+            elif kind == "A":
+                b, g = st[1], st[2]
+                bank = open_bank(("A", b, g))
+                pcols = slice((b % 2) * P, (b % 2 + 1) * P)
+                for t in range(4):
+                    cols = slice(t * P, (t + 1) * P)
+                    nc.tensor.matmul_mx(out=bank[:, cols], lhsT=cq[g][0][:, cols].bitcast(FP8X4),
+                                        lhsT_scale=cq[g][1][:, cols],
+                                        rhs=pq[b // 2][0][:, pcols].bitcast(FP8X4), rhs_scale=pq[b // 2][1][:, pcols],
+                                        start=True, stop=True)
+            elif kind == "RA":
+                b, g = st[1], st[2]
+                first, j, cnt = agroup[(b, g)]
+                if first not in ab:
+                    ab[first] = keep.tile([P, cnt * 512], BF16, name="ab%d_%d" % first, align_bytes=64)
+                dst = ab[first][:, 512 * j:512 * (j + 1)].rearrange("m (e t) -> m e t", t=4)
+                src = banks[("A", b, g)][:].rearrange("m (t e) -> m e t", t=4)
+                close_bank(("A", b, g))
+                if st[3] == "S":
+                    nc.scalar.activation(out=dst, in_=src, func=ACT.Relu)
+                else:
+                    nc.vector.tensor_scalar_max(out=dst, in0=src, scalar1=0.0)
+            elif kind == "QA":
+                first = st[1][0]
+                aq[first] = quantise("aq%d_%d" % first, ab[first][:], P * len(st[1]))
+            elif kind == "O":
+                b, g = st[1], st[2]
+                if g == 0:
+                    open_bank(("O", b))
+                first, j, cnt = agroup[(b, g)]
+                cols = slice(j * P, (j + 1) * P)
+                nc.tensor.matmul_mx(out=banks[("O", b)][:], lhsT=aq[first][0][:, cols].bitcast(FP8X4),
+                                    lhsT_scale=aq[first][1][:, cols], rhs=vcodes[g][:].bitcast(FP8X4),
+                                    rhs_scale=vscales[g][:], start=(g == 0), stop=(g == 3))
+            else:
+                b = st[1]
+                res = stage.tile([P, 512], F32, name="res", tag="res", bufs=8)
+                copy_out(st[2], res[:], banks[("O", b)][:])
+                nc.sync.dma_start(out=out_rows[:, b, :], in_=res[:])
+                close_bank(("O", b))

@@ -12,120 +12,112 @@ FP8X4 = mybir.dt.float8_e4m3fn_x4
 FP4X4 = mybir.dt.float4_e2m1fn_x4
 ACT = mybir.ActivationFunctionType
 
-E, J, N, PK, R = 1024, 512, 2048, 1024, 512
-FLOPS = 2 * N * PK * R + 2 * E * J * N + 2 * E * N * R
-P = 128
+EVENTS, BASIS, SUBJECTS, COVARIATES, MODELS = 1024, 512, 2048, 1024, 512
+FLOPS = 2 * SUBJECTS * (COVARIATES * MODELS + EVENTS * BASIS + EVENTS * MODELS)
 
+P = 128
+PACK = 4
+BANK = 512
+BANKS = 8
+GROUPS = SUBJECTS // (P * PACK)
+BLOCKS = EVENTS // P
+BF16_ONE_PAIR = 0x3F803F80
+WARM_PASSES = 14
+
+READER = {"TX": "EX", "TP": "EP", "H": "EXP", "A": "RA"}
+
+X_SETS = dict([(0, [0]), (1, [1])] + [(s, [s, s + 1]) for s in range(2, 16, 2)])
+X_SINGLE_LOADS = 4
+A_SETS = [[(0, g), (1, g)] for g in range(GROUPS)] + [[(b, g) for g in range(GROUPS)] for b in range(2, BLOCKS)]
+PIECES = [(b, 0, MODELS) for b in range(BLOCKS - 1)] + [(BLOCKS - 1, h * MODELS // 2, MODELS // 2) for h in range(2)]
+
+LOAD_ORDER = (
+    "x0 x1 x2 bs x3 bw x4 c0 p1 p3 c1 p0 p2 c2 x6 c3 x8 x10 z0 x14 x12 z1 z3 z2 "
+)
 TENSOR_ORDER = (
-    "TX0 TX1 TX2 TX3 H1 H0 TX4 TX5 H2 TP1 TP2 TP0 H4 A2.0 "
-    "H3 A3.0 H5 A5.0 TX6 TX7 TX9 TX8 A1.1 A3.1 A3.2 A0.1 TP3 TX11 "
-    "TX10 H6 A1.2 H7 A1.0 H8 A0.0 A4.0 A3.3 A2.1 TX12 TX15 TX13 TX14 "
-    "A4.1 A2.2 A2.3 A6.3 H10 A4.2 H11 A1.3 H9 A4.3 O2.0 A0.2 H14 H12 "
-    "O0.0 H13 H15 O1.0 O3.0 O1.1 A0.3 O0.1 A7.2 O2.1 A6.1 O3.1 A6.0 A5.1 "
-    "A7.1 O0.2 O1.2 O2.2 A7.3 O3.2 A6.2 O4.0 A5.3 O4.1 A7.0 A5.2 O4.2 O3.3 "
-    "O1.3 O6.0 O2.3 O6.1 O6.2 O6.3 O4.3 O7.0 O5.0 O7.1 O0.3 O7.2 O7.3 O5.1 "
-    "O5.2 O5.3 "
+    "TX0 TX1 TX2 TX3 H0 H1 TX4 TX5 H2 H3 TP1 TP3 H4 H5 TP0 TP2 "
+    "A3.0 A2.0 A7.0 A2.1 A3.1 TX6 TX7 A0.0 A1.0 A4.0 A5.0 A6.0 A1.1 A3.2 TX8 TX9 "
+    "TX10 TX11 A0.1 H6 A0.2 H7 A2.2 A2.3 A3.3 TX12 TX13 TX14 TX15 H8 H9 A1.2 "
+    "H10 H11 A4.1 H12 O0.0 A5.1 H13 H14 A6.1 A7.1 O2.0 H15 A4.2 O1.0 O1.1 A5.3 "
+    "O0.1 A5.2 O2.1 A6.2 A6.3 O2.2 A7.2 A0.3 O1.2 A1.3 O3.0 O0.2 A4.3 O3.1 A7.3 O3.2 "
+    "O6.0 O6.1 O2.3 O6.2 O3.3 O5.0 O0.3 O6.3 O5.1 O5.2 O5.3 O4.0 O4.1 O1.3 O4.2 O4.3 "
+    "O7.0 O7.1 O7.2 O7.3 O8.0 O8.1 O8.2 O8.3 "
 )
 VECTOR_ORDER = (
-    "EX0 QX0 QX2 IC0 QX4 QC0 QP1 IC1 QP2 IC2 QC1 QP0 QC2 IC3 "
-    "QX6 QX8 QC3 MUL0.1 EP3 QX10 RA1.0 RA3.1 MUL0.0 QA0.1 RA2.1 QP3 QV0.0 MUL1.0 "
-    "RA2.3 EX14 QA2.0 QX14 QX12 QA0.0 MUL1.1 QA3.0 QV1.0 MUL2.0 MUL2.1 QA0.2 QV2.0 QA4.0 "
-    "MUL3.1 MUL3.0 QA0.3 QV3.0 QA6.0 QA7.0 QA5.0 EO7 "
+    "QX0 QX1 QX2 IC0 QX4 QC0 IC1 QP1 QP3 QC1 IC2 RA2.0 QP0 QP2 "
+    "QC2 IC3 QX6 QC3 RA6.0 RA1.1 QA0 RA3.2 MUL0.0 QX8 MUL0.1 QX10 RA3.3 QV0 "
+    "MUL1.0 EX12 QA1 QX14 QX12 QA4 QA2 MUL1.1 MUL2.0 QV1 MUL2.1 QA5 QV2 RA5.3 "
+    "MUL3.0 MUL3.1 QA8 QV3 QA7 QA3 QA6 QA9 EO8 "
 )
-LOAD_ORDER = "x0 x1 x2 bw bs x4 c0 p1 p2 p0 c1 c2 x6 x8 c3 p3 x10 z0 x14 x12 z2 z1 z3"
-WARM = 18
 
 
-def parse(name):
-    kind = "".join([ch for ch in name if ch in "ABCEHILMOPQRTUVX"])
-    return kind, [int(v) for v in name.replace(kind, "").split(".")]
+def parse(step):
+    kind = "".join([ch for ch in step if ch not in "0123456789."])
+    return kind, tuple(int(v) for v in step.replace(kind, "").split("."))
 
 
-def a_group(b, g):
-    if b < 2:
-        return [(0, g), (1, g)]
-    return [(b, k) for k in range(4)]
+def x_set_of(slot):
+    return [first for first, slots in X_SETS.items() if slot in slots][0]
 
 
-def needs(name):
-    kind, a = parse(name)
-    if kind in ("TX", "TP", "IC"):
-        return []
-    if kind == "EX":
-        return ["TX%d" % a[0]]
+def a_set_of(block, group):
+    return [i for i, tiles in enumerate(A_SETS) if (block, group) in tiles][0]
+
+
+def inputs_of(kind, at):
+    if kind in ("EX", "EP", "EXP", "RA"):
+        return [(writer, at) for writer, reader in READER.items() if reader == kind]
+    if kind == "EO":
+        return [("O", (at[0], GROUPS - 1))]
     if kind == "QX":
-        return ["EX%d" % a[0], "EX%d" % (a[0] + 1)]
+        return [("EX", (s,)) for s in X_SETS[at[0]]]
     if kind == "H":
-        return ["QX%d" % (a[0] - a[0] % 2)]
-    if kind == "EXP":
-        return ["H%d" % a[0]]
+        return [("QX", (x_set_of(at[0]),))]
     if kind == "MUL":
-        return ["EXP%d" % (4 * a[0] + t) for t in range(4)]
+        return [("EXP", (PACK * at[0] + t,)) for t in range(PACK)]
     if kind == "QV":
-        return ["MUL%d.0" % a[0], "MUL%d.1" % a[0]]
+        return [("MUL", (at[0], h)) for h in range(2)]
     if kind == "QC":
-        return ["IC%d" % a[0]]
-    if kind == "EP":
-        return ["TP%d" % a[0]]
+        return [("IC", at)]
     if kind == "QP":
-        return ["EP%d" % a[0]]
+        return [("EP", at)]
     if kind == "A":
-        return ["QP%d" % (a[0] // 2), "QC%d" % a[1]]
-    if kind == "RA":
-        return ["A%d.%d" % (a[0], a[1])]
+        return [("QP", (at[0] // 2,)), ("QC", (at[1],))]
     if kind == "QA":
-        return ["RA%d.%d" % key for key in a_group(a[0], a[1])]
+        return [("RA", tile) for tile in A_SETS[at[0]]]
     if kind == "O":
-        return ["QA%d.%d" % a_group(a[0], a[1])[0], "QV%d.0" % a[1]]
-    return ["O%d.3" % a[0]]
+        return [("QA", (a_set_of(PIECES[at[0]][0], at[1]),)), ("QV", (at[1],))]
+    return []
 
 
 def program():
-    scalar_order = []
-    for name in TENSOR_ORDER.split():
-        kind, a = parse(name)
-        if kind == "O":
-            reader = "EO%d" % a[0] if a[1] == 3 else None
-        else:
-            reader = {"TX": "EX", "TP": "EP", "H": "EXP", "A": "RA"}[kind] + name.replace(kind, "")
-        if reader is not None and reader not in VECTOR_ORDER.split():
-            scalar_order.append(reader)
-    queues = [scalar_order, VECTOR_ORDER.split(), TENSOR_ORDER.split()]
-    heads = [0, 0, 0]
-    emitted = set()
-    free_banks = 8
-    steps = []
-    total = sum(len(q) for q in queues)
-    while_guard = range(total)
-    for turn in while_guard:
-        pick = None
-        for k in range(3):
-            if pick is None and heads[k] < len(queues[k]):
-                name = queues[k][heads[k]]
-                kind, a = parse(name)
-                opens = k == 2 and (kind != "O" or a[1] == 0)
-                if all(d in emitted for d in needs(name)) and (free_banks > 0 or not opens):
-                    pick = k
-        name = queues[pick][heads[pick]]
-        heads[pick] = heads[pick] + 1
-        emitted.add(name)
-        kind, a = parse(name)
-        eng = "SVT"[pick]
-        if pick == 2 and (kind != "O" or a[1] == 0):
-            free_banks -= 1
-        if kind in ("EX", "EP", "EXP", "RA", "EO"):
-            free_banks += 1
-        if kind == "QX":
-            steps.append((kind, [a[0], a[0] + 1]))
-        elif kind == "QA":
-            steps.append((kind, a_group(a[0], a[1])))
-        elif kind == "MUL":
-            steps.append((kind, a[0], a[1], 2))
-        elif kind == "QV":
-            steps.append((kind, a[0], [0, 1], 2))
-        else:
-            steps.append(tuple([kind] + a + [eng]))
-    return steps
+    tensor_steps = [parse(step) for step in TENSOR_ORDER.split()]
+    vector_steps = [parse(step) for step in VECTOR_ORDER.split()]
+    readers = []
+    for kind, at in tensor_steps:
+        if kind in READER:
+            readers.append((READER[kind], at))
+        elif at[1] == GROUPS - 1:
+            readers.append(("EO", at[:1]))
+    scalar_steps = [step for step in readers if step not in vector_steps]
+
+    queues = [scalar_steps, vector_steps, tensor_steps]
+    written, text, free_banks = set(), [], BANKS
+    for count in range(sum(len(queue) for queue in queues)):
+        ready = []
+        for queue in queues:
+            if queue and all(step in written for step in inputs_of(*queue[0])):
+                kind, at = queue[0]
+                opens_bank = kind in READER or (kind == "O" and at[1] == 0)
+                if free_banks > 0 or not opens_bank:
+                    ready.append((queue, opens_bank))
+        queue, opens_bank = ready[0]
+        step = queue[0]
+        queue.remove(step)
+        written.add(step)
+        text.append((step[0], step[1], queue is scalar_steps))
+        free_banks += (1 if step in readers else 0) - (1 if opens_bank else 0)
+    return text
 
 
 def tile_cox_risk_sums_s11_kernel(tc, x, b_words, b_scales, z, phi, c, out):
@@ -136,199 +128,185 @@ def tile_cox_risk_sums_s11_kernel(tc, x, b_words, b_scales, z, phi, c, out):
         psum = ctx.enter_context(tc.psum_pool(name="psum", bufs=1))
         ctx.enter_context(tc.manual_schedule())
 
-        x_rows = x.rearrange("(g m t) k -> g m (t k)", g=4, t=4)
-        z_rows = z.rearrange("(g m t) r -> g m (t r)", g=4, t=4)
-        c_rows = c.rearrange("(p j) n -> p j n", j=4)
-        phi_rows = phi.rearrange("(p b) j -> p (b j)", b=8)
-        out_rows = out.rearrange("(p b) r -> p b r", b=8)
-
-        ident = keep.tile([P, P], F32, name="ident")
-        make_identity(nc, ident[:])
-        warm = keep.tile([P, 8], F32, name="warm")
-        bs = keep.tile([P, 1024], U8, name="bs", align_bytes=64)
-        nc.vector.memset(bs[:].bitcast(I32), 0)
-        nc.vector.memset(warm[:, 0:4], 0.0)
-        nc.scalar.activation(out=warm[:, 4:5], in_=warm[:, 0:1], func=ACT.Exp)
-        bw = keep.tile([P, 2048], U8, name="bw", align_bytes=64)
-
-        xraw = [keep.tile([P, 2048], BF16, name="x%d" % s, align_bytes=64) for s in range(8)]
-        zraw = [keep.tile([P, 2048], BF16, name="z%d" % g, align_bytes=64) for g in range(4)]
-        craw = [keep.tile([P, 2048], BF16, name="c%d" % g, align_bytes=64) for g in range(4)]
-        praw = [keep.tile([P, 1024], BF16, name="phi%d" % k, align_bytes=64) for k in range(4)]
-        for item in LOAD_ORDER.split():
-            if item == "bw":
-                nc.sync.dma_start(out=bw[:].bitcast(I32).rearrange("p (h n) -> p h n", h=2),
-                                  in_=b_words.bitcast(I32).rearrange("h p n -> p h n"))
-            elif item == "bs":
-                for q in range(4):
-                    nc.sync.dma_start(
-                        out=bs[32 * q:32 * q + 4, :].bitcast(I32).rearrange("r (h n) -> r h n", h=2),
-                        in_=b_scales.bitcast(I32)[:, 4 * q:4 * q + 4, :].rearrange("h r n -> r h n"))
-            else:
-                kind, i = item[0], int(item[1:])
-                if kind == "x":
-                    cnt = 1 if i < 2 else 2
-                    g, t0 = divmod(i, 4)
-                    nc.sync.dma_start(out=xraw[i // 2][:, (i % 2) * 1024:(i % 2 + cnt) * 1024],
-                                      in_=x_rows[g, :, t0 * 1024:(t0 + cnt) * 1024])
-                elif kind == "z":
-                    nc.sync.dma_start(out=zraw[i][:], in_=z_rows[i])
-                elif kind == "c":
-                    nc.sync.dma_start(out=craw[i][:].rearrange("p (j n) -> p j n", j=4), in_=c_rows[:, :, i * 512:(i + 1) * 512])
-                else:
-                    nc.sync.dma_start(out=praw[i][:], in_=phi_rows[:, i * 1024:(i + 1) * 1024])
-
-        free = list(range(8))
-        banks = {}
-        bank_index = {}
-
-        def open_bank(key):
-            index = free[0]
-            free.remove(index)
-            bank_index[key] = index
-            banks[key] = psum.tile([P, 512], F32, name="bank%d" % index, tag="bank%d" % index)
-            return banks[key]
-
-        def close_bank(key):
-            free.append(bank_index[key])
-
-        def copy_out(eng, dst, src):
-            if eng == "S":
-                nc.scalar.copy(out=dst, in_=src)
-            else:
-                nc.vector.tensor_copy(out=dst, in_=src)
-
-        def quantise(name, src, words):
+        def quantise(name, src):
+            words = src.shape[1] // PACK
             codes = keep.tile([P, words], U32, name=name + "_codes", align_bytes=64)
             scales = keep.tile([P, words], U8, name=name + "_scales", align_bytes=64)
             nc.vector.quantize_mx(out=codes[:].bitcast(FP8X4), scales=scales[:], in_=src)
             return codes, scales
 
-        if WARM:
-            ones = keep.tile([P, 512], BF16, name="ones", align_bytes=64)
-            nc.vector.memset(ones[:].bitcast(I32), 0x3F803F80)
-            wcodes, wscales = quantise("warm", ones[:], P)
-            wbank = psum.tile([P, 512], F32, name="bank7", tag="bank7")
-            for i in range(WARM):
-                nc.tensor.matmul_mx(out=wbank[:, (i % 4) * P:(i % 4 + 1) * P], lhsT=wcodes[:].bitcast(FP8X4), lhsT_scale=wscales[:],
-                                    rhs=wcodes[:].bitcast(FP8X4), rhs_scale=wscales[:], start=True, stop=True)
+        def mx_pass(dst, lhs, lhs_cols, rhs, rhs_cols, start, stop):
+            nc.tensor.matmul_mx(out=dst, lhsT=lhs[0][:, lhs_cols].bitcast(FP8X4), lhsT_scale=lhs[1][:, lhs_cols],
+                                rhs=rhs[0][:, rhs_cols].bitcast(FP8X4), rhs_scale=rhs[1][:, rhs_cols],
+                                start=start, stop=stop)
 
-        steps = program()
-        xgroup, agroup = {}, {}
-        for st in steps:
-            if st[0] == "QX":
-                for j, u in enumerate(st[1]):
-                    xgroup[u] = (st[1][0], j, len(st[1]))
-            if st[0] == "QA":
-                for j, key in enumerate(st[1]):
-                    agroup[key] = (st[1][0], j, len(st[1]))
-        xg, xq, ex, vb, cg, cq, pg, pq, ab, aq = {}, {}, {}, {}, {}, {}, {}, {}, {}, {}
-        vcodes = [keep.tile([P, 512], U32, name="vcodes%d" % g, align_bytes=64) for g in range(4)]
-        vscales = [keep.tile([P, 512], U8, name="vscales%d" % g, align_bytes=64) for g in range(4)]
+        def columns(index, width):
+            return slice(index * width, (index + 1) * width)
 
-        def transpose4(key, tl, j):
+        ident = keep.tile([P, P], F32, name="ident")
+        make_identity(nc, ident[:])
+        table_probe = keep.tile([P, 8], F32, name="table_probe")
+        b_scale_plane = keep.tile([P, 2 * MODELS], U8, name="b_scale_plane", align_bytes=64)
+        ones = keep.tile([P, PACK * P], BF16, name="ones", align_bytes=64)
+        nc.vector.memset(ones[:].bitcast(I32), BF16_ONE_PAIR)
+        nc.vector.memset(table_probe[:, 0:4], 0.0)
+        ones_mx = quantise("ones", ones[:])
+        nc.vector.memset(b_scale_plane[:].bitcast(I32), 0)
+        nc.scalar.activation(out=table_probe[:, 4:5], in_=table_probe[:, 0:1], func=ACT.Exp)
+        b_codes = keep.tile([P, 2 * 2 * MODELS], U8, name="b_codes", align_bytes=64)
+
+        x_rows = x.rearrange("(g m t) k -> g m (t k)", g=GROUPS, t=PACK)
+        z_rows = z.rearrange("(g m t) r -> g m (t r)", g=GROUPS, t=PACK)
+        c_rows = c.rearrange("(p j) n -> p j n", j=PACK)
+        phi_rows = phi.rearrange("(p b) j -> p (b j)", b=BLOCKS)
+        out_rows = out.rearrange("(p b) r -> p b r", b=BLOCKS)
+
+        x_tiles = [keep.tile([P, 2 * COVARIATES], BF16, name="x%d" % i, align_bytes=64) for i in range(8)]
+        phi_tiles = [keep.tile([P, 2 * BASIS], BF16, name="phi%d" % i, align_bytes=64) for i in range(BLOCKS // 2)]
+        z_tiles = [keep.tile([P, PACK * MODELS], BF16, name="z%d" % g, align_bytes=64) for g in range(GROUPS)]
+        cv_tiles = [keep.tile([P, PACK * BANK], BF16, name="cv%d" % g, align_bytes=64) for g in range(GROUPS)]
+        a_tiles = [keep.tile([P, len(tiles) * BANK], BF16, name="a%d" % i, align_bytes=64)
+                   for i, tiles in enumerate(A_SETS)]
+
+        for load in LOAD_ORDER.split():
+            if load == "bw":
+                nc.sync.dma_start(out=b_codes[:].bitcast(I32).rearrange("p (h n) -> p h n", h=2),
+                                  in_=b_words.bitcast(I32).rearrange("h p n -> p h n"))
+            elif load == "bs":
+                for q in range(4):
+                    nc.sync.dma_start(
+                        out=b_scale_plane[32 * q:32 * q + 4, :].bitcast(I32).rearrange("r (h n) -> r h n", h=2),
+                        in_=b_scales.bitcast(I32)[:, 4 * q:4 * q + 4, :].rearrange("h r n -> r h n"))
+            else:
+                kind, (i,) = parse(load)
+                if kind == "x":
+                    width = COVARIATES * (1 if i < X_SINGLE_LOADS else 2)
+                    g, t = divmod(i, PACK)
+                    nc.sync.dma_start(out=x_tiles[i // 2][:, (i % 2) * COVARIATES:(i % 2) * COVARIATES + width],
+                                      in_=x_rows[g, :, t * COVARIATES:t * COVARIATES + width])
+                elif kind == "z":
+                    nc.sync.dma_start(out=z_tiles[i][:], in_=z_rows[i])
+                elif kind == "c":
+                    nc.sync.dma_start(out=cv_tiles[i][:].rearrange("p (j n) -> p j n", j=PACK),
+                                      in_=c_rows[:, :, columns(i, BANK)])
+                else:
+                    nc.sync.dma_start(out=phi_tiles[i][:], in_=phi_rows[:, columns(i, 2 * BASIS)])
+
+        free_banks = list(range(BANKS))
+        bank_of, bank_index = {}, {}
+
+        def new_bank(index):
+            return psum.tile([P, BANK], F32, name="bank%d" % index, tag="bank%d" % index)
+
+        def open_bank(key):
+            bank_index[key] = free_banks[0]
+            free_banks.remove(bank_index[key])
+            bank_of[key] = new_bank(bank_index[key])
+            return bank_of[key]
+
+        def close_bank(key):
+            free_banks.append(bank_index[key])
+            return bank_of[key]
+
+        def copy(on_scalar, dst, src):
+            if on_scalar:
+                nc.scalar.copy(out=dst, in_=src)
+            else:
+                nc.vector.tensor_copy(out=dst, in_=src)
+
+        def transpose_words(key, words):
             bank = open_bank(key)
-            words = tl[:].bitcast(F32)
             for h in range(2):
                 for u in range(2):
-                    w0 = 512 * j + 256 * h
-                    nc.tensor.transpose(bank[:, (2 * h + u) * P:(2 * h + u + 1) * P],
-                                        words[:, w0 + u:w0 + 256:2], ident[:])
+                    nc.tensor.transpose(bank[:, columns(2 * h + u, P)], words[:, 2 * P * h + u:2 * P * (h + 1):2],
+                                        ident[:])
 
-        def evacuate4(eng, key, tl, j):
-            close_bank(key)
-            copy_out(eng, tl[:].bitcast(F32)[:, 512 * j:512 * (j + 1)].rearrange("q (h m u) -> q h m u", h=2, u=2),
-                     banks[key][:].rearrange("q (h u m) -> q h m u", h=2, u=2))
+        def copy_words_out(key, words, on_scalar):
+            copy(on_scalar, words.rearrange("q (h m u) -> q h m u", h=2, u=2),
+                 close_bank(key)[:].rearrange("q (h u m) -> q h m u", h=2, u=2))
 
-        for st in steps:
-            kind = st[0]
+        def x_words(slot):
+            return x_tiles[slot // 2][:].bitcast(F32)[:, columns(slot % 2, BANK)]
+
+        warm_bank = new_bank(BANKS - 1)
+        for i in range(WARM_PASSES):
+            mx_pass(warm_bank[:, columns(i % PACK, P)], ones_mx, columns(0, P), ones_mx, columns(0, P), True, True)
+
+        x_mx, phi_mx, c_mx, v_mx, a_mx, hazard, c_grouped = {}, {}, {}, {}, {}, {}, {}
+        for kind, at, on_scalar in program():
             if kind == "TX":
-                transpose4(("X", st[1]), xraw[st[1] // 2], st[1] % 2)
+                transpose_words(("X", at), x_words(at[0]))
             elif kind == "EX":
-                evacuate4(st[2], ("X", st[1]), xraw[st[1] // 2], st[1] % 2)
+                copy_words_out(("X", at), x_words(at[0]), on_scalar)
             elif kind == "QX":
-                first = st[1][0]
-                xq[first] = quantise("xq%d" % first, xraw[first // 2][:], 256 * len(st[1]))
+                first = (at[0] % 2) * COVARIATES
+                x_mx[at[0]] = quantise("xq%d" % at,
+                                       x_tiles[at[0] // 2][:, first:first + len(X_SETS[at[0]]) * COVARIATES])
             elif kind == "H":
-                first, j, cnt = xgroup[st[1]]
-                codes, scales = xq[first]
-                bank = open_bank(("H", st[1]))
+                first = x_set_of(at[0])
+                codes, scales = x_mx[first]
+                bank = open_bank(("H", at))
                 for h in range(2):
-                    cols = slice((2 * j + h) * P, (2 * j + h + 1) * P)
+                    cols = columns(2 * (at[0] - first) + h, P)
                     nc.tensor.matmul_mx(out=bank[:], lhsT=codes[:, cols].bitcast(FP8X4), lhsT_scale=scales[:, cols],
-                                        rhs=bw[:, 1024 * h:1024 * (h + 1)].bitcast(FP4X4),
-                                        rhs_scale=bs[:, 512 * h:512 * (h + 1)], start=(h == 0), stop=(h == 1))
+                                        rhs=b_codes[:, columns(h, 2 * MODELS)].bitcast(FP4X4),
+                                        rhs_scale=b_scale_plane[:, columns(h, MODELS)], start=(h == 0), stop=(h == 1))
             elif kind == "EXP":
-                g, t = divmod(st[1], 4)
-                if g not in ex:
-                    ex[g] = stage.tile([P, 2048], F32, name="ex", tag="ex", bufs=4, align_bytes=64)
-                nc.scalar.activation(out=ex[g][:, 512 * t:512 * (t + 1)], in_=banks[("H", st[1])][:], func=ACT.Exp)
-                close_bank(("H", st[1]))
+                g, t = divmod(at[0], PACK)
+                if g not in hazard:
+                    hazard[g] = stage.tile([P, PACK * MODELS], F32, name="hazard", tag="hazard", bufs=GROUPS,
+                                           align_bytes=64)
+                nc.scalar.activation(out=hazard[g][:, columns(t, MODELS)], in_=close_bank(("H", at))[:], func=ACT.Exp)
             elif kind == "MUL":
-                g, h, nh = st[1], st[2], st[3]
-                vb[g] = craw[g]
-                cs = slice(h * (128 // nh), (h + 1) * (128 // nh))
+                g, half = at[0], columns(at[1], MODELS // (2 * 4))
                 nc.vector.tensor_tensor(
-                    out=vb[g][:].rearrange("p (c i t) -> p c t i", i=4, t=4)[:, cs],
-                    in0=ex[g][:].rearrange("p (t c i) -> p c t i", i=4, t=4)[:, cs],
-                    in1=zraw[g][:].rearrange("p (t c i) -> p c t i", i=4, t=4)[:, cs],
+                    out=cv_tiles[g][:].rearrange("p (c i t) -> p c t i", i=4, t=PACK)[:, half],
+                    in0=hazard[g][:].rearrange("p (t c i) -> p c t i", i=4, t=PACK)[:, half],
+                    in1=z_tiles[g][:].rearrange("p (t c i) -> p c t i", i=4, t=PACK)[:, half],
                     op=mybir.AluOpType.mult)
             elif kind == "QV":
-                g, hs, nh = st[1], st[2], st[3]
-                w = 512 // nh
-                lo, hi = hs[0] * w, (hs[-1] + 1) * w
-                nc.vector.quantize_mx(out=vcodes[g][:, lo:hi].bitcast(FP8X4), scales=vscales[g][:, lo:hi],
-                                      in_=vb[g][:, 4 * lo:4 * hi])
+                v_mx[at[0]] = quantise("vq%d" % at, cv_tiles[at[0]][:])
             elif kind == "IC":
-                g = st[1]
-                cg[g] = stage.tile([P, 2048], BF16, name="cg", tag="cg", bufs=2, align_bytes=64)
-                copy_out(st[2], cg[g][:].rearrange("p (t a b j) -> p a t b j", t=4, b=2, j=4),
-                         craw[g][:].rearrange("p (j a b t) -> p a t b j", j=4, b=2, t=4))
+                c_grouped[at[0]] = stage.tile([P, PACK * BANK], BF16, name="c_grouped", tag="c_grouped",
+                                              align_bytes=64)
+                nc.vector.tensor_copy(
+                    out=c_grouped[at[0]][:].rearrange("p (t a d j) -> p a t d j", t=PACK, d=2, j=PACK),
+                    in_=cv_tiles[at[0]][:].rearrange("p (j a d t) -> p a t d j", j=PACK, d=2, t=PACK))
             elif kind == "QC":
-                cq[st[1]] = quantise("cq%d" % st[1], cg[st[1]][:], 512)
+                c_mx[at[0]] = quantise("cq%d" % at, c_grouped[at[0]][:])
             elif kind == "TP":
-                transpose4(("P", st[1]), praw[st[1]], 0)
+                transpose_words(("P", at), phi_tiles[at[0]][:].bitcast(F32))
             elif kind == "EP":
-                evacuate4(st[2], ("P", st[1]), praw[st[1]], 0)
+                copy_words_out(("P", at), phi_tiles[at[0]][:].bitcast(F32), on_scalar)
             elif kind == "QP":
-                pq[st[1]] = quantise("pq%d" % st[1], praw[st[1]][:], 256)
+                phi_mx[at[0]] = quantise("pq%d" % at, phi_tiles[at[0]][:])
             elif kind == "A":
-                b, g = st[1], st[2]
-                bank = open_bank(("A", b, g))
-                pcols = slice((b % 2) * P, (b % 2 + 1) * P)
-                for t in range(4):
-                    cols = slice(t * P, (t + 1) * P)
-                    nc.tensor.matmul_mx(out=bank[:, cols], lhsT=cq[g][0][:, cols].bitcast(FP8X4),
-                                        lhsT_scale=cq[g][1][:, cols],
-                                        rhs=pq[b // 2][0][:, pcols].bitcast(FP8X4), rhs_scale=pq[b // 2][1][:, pcols],
-                                        start=True, stop=True)
+                b, g = at
+                bank = open_bank(("A", at))
+                for t in range(PACK):
+                    mx_pass(bank[:, columns(t, P)], c_mx[g], columns(t, P), phi_mx[b // 2], columns(b % 2, P),
+                            True, True)
             elif kind == "RA":
-                b, g = st[1], st[2]
-                first, j, cnt = agroup[(b, g)]
-                if first not in ab:
-                    ab[first] = keep.tile([P, cnt * 512], BF16, name="ab%d_%d" % first, align_bytes=64)
-                dst = ab[first][:, 512 * j:512 * (j + 1)].rearrange("m (e t) -> m e t", t=4)
-                src = banks[("A", b, g)][:].rearrange("m (t e) -> m e t", t=4)
-                close_bank(("A", b, g))
-                if st[3] == "S":
+                a_set = a_set_of(*at)
+                dst = a_tiles[a_set][:, columns(A_SETS[a_set].index(at), BANK)]
+                dst = dst.rearrange("m (c i t) -> m c t i", i=2, t=PACK)
+                src = close_bank(("A", at))[:].rearrange("m (t c i) -> m c t i", i=2, t=PACK)
+                if on_scalar:
                     nc.scalar.activation(out=dst, in_=src, func=ACT.Relu)
                 else:
                     nc.vector.tensor_scalar_max(out=dst, in0=src, scalar1=0.0)
             elif kind == "QA":
-                first = st[1][0]
-                aq[first] = quantise("aq%d_%d" % first, ab[first][:], P * len(st[1]))
+                a_mx[at[0]] = quantise("aq%d" % at, a_tiles[at[0]][:])
             elif kind == "O":
-                b, g = st[1], st[2]
+                piece, g = at
+                b, first, width = PIECES[piece]
                 if g == 0:
-                    open_bank(("O", b))
-                first, j, cnt = agroup[(b, g)]
-                cols = slice(j * P, (j + 1) * P)
-                nc.tensor.matmul_mx(out=banks[("O", b)][:], lhsT=aq[first][0][:, cols].bitcast(FP8X4),
-                                    lhsT_scale=aq[first][1][:, cols], rhs=vcodes[g][:].bitcast(FP8X4),
-                                    rhs_scale=vscales[g][:], start=(g == 0), stop=(g == 3))
+                    open_bank(("O", piece))
+                a_set = a_set_of(b, g)
+                mx_pass(bank_of[("O", piece)][:, 0:width], a_mx[a_set], columns(A_SETS[a_set].index((b, g)), P),
+                        v_mx[g], slice(first, first + width), g == 0, g == GROUPS - 1)
             else:
-                b = st[1]
-                res = stage.tile([P, 512], F32, name="res", tag="res", bufs=8)
-                copy_out(st[2], res[:], banks[("O", b)][:])
-                nc.sync.dma_start(out=out_rows[:, b, :], in_=res[:])
-                close_bank(("O", b))
+                b, first, width = PIECES[at[0]]
+                result = stage.tile([P, width], F32, name="result", tag="result", bufs=BLOCKS)
+                copy(on_scalar, result[:], close_bank(("O", at[0]))[:, 0:width])
+                nc.sync.dma_start(out=out_rows[:, b, first:first + width], in_=result[:])

from contextlib import ExitStack

import concourse.mybir as mybir
from concourse.masks import make_identity

F32 = mybir.dt.float32
BF16 = mybir.dt.bfloat16
I32 = mybir.dt.int32
U32 = mybir.dt.uint32
U8 = mybir.dt.uint8
FP8X4 = mybir.dt.float8_e4m3fn_x4
FP4X4 = mybir.dt.float4_e2m1fn_x4
ACT = mybir.ActivationFunctionType

EVENTS, BASIS, SUBJECTS, COVARIATES, MODELS = 1024, 512, 2048, 1024, 512
FLOPS = 2 * SUBJECTS * (COVARIATES * MODELS + EVENTS * BASIS + EVENTS * MODELS)

P = 128
PACK = 4
BANK = 512
BANKS = 8
GROUPS = SUBJECTS // (P * PACK)
BLOCKS = EVENTS // P
BF16_ONE_PAIR = 0x3F803F80
WARM_PASSES = 14

READER = {"TX": "EX", "TP": "EP", "H": "EXP", "A": "RA"}

X_SETS = dict([(0, [0]), (1, [1])] + [(s, [s, s + 1]) for s in range(2, 16, 2)])
X_SINGLE_LOADS = 4
A_SETS = [[(0, g), (1, g)] for g in range(GROUPS)] + [[(b, g) for g in range(GROUPS)] for b in range(2, BLOCKS)]
PIECES = [(b, 0, MODELS) for b in range(BLOCKS - 1)] + [(BLOCKS - 1, h * MODELS // 2, MODELS // 2) for h in range(2)]

LOAD_ORDER = (
    "x0 x1 x2 bs x3 bw x4 c0 p1 p3 c1 p0 p2 c2 x6 c3 x8 x10 z0 x14 x12 z1 z3 z2 "
)
TENSOR_ORDER = (
    "TX0 TX1 TX2 TX3 H0 H1 TX4 TX5 H2 H3 TP1 TP3 H4 H5 TP0 TP2 "
    "A3.0 A2.0 A7.0 A2.1 A3.1 TX6 TX7 A0.0 A1.0 A4.0 A5.0 A6.0 A1.1 A3.2 TX8 TX9 "
    "TX10 TX11 A0.1 H6 A0.2 H7 A2.2 A2.3 A3.3 TX12 TX13 TX14 TX15 H8 H9 A1.2 "
    "H10 H11 A4.1 H12 O0.0 A5.1 H13 H14 A6.1 A7.1 O2.0 H15 A4.2 O1.0 O1.1 A5.3 "
    "O0.1 A5.2 O2.1 A6.2 A6.3 O2.2 A7.2 A0.3 O1.2 A1.3 O3.0 O0.2 A4.3 O3.1 A7.3 O3.2 "
    "O6.0 O6.1 O2.3 O6.2 O3.3 O5.0 O0.3 O6.3 O5.1 O5.2 O5.3 O4.0 O4.1 O1.3 O4.2 O4.3 "
    "O7.0 O7.1 O7.2 O7.3 O8.0 O8.1 O8.2 O8.3 "
)
VECTOR_ORDER = (
    "QX0 QX1 QX2 IC0 QX4 QC0 IC1 QP1 QP3 QC1 IC2 RA2.0 QP0 QP2 "
    "QC2 IC3 QX6 QC3 RA6.0 RA1.1 QA0 RA3.2 MUL0.0 QX8 MUL0.1 QX10 RA3.3 QV0 "
    "MUL1.0 EX12 QA1 QX14 QX12 QA4 QA2 MUL1.1 MUL2.0 QV1 MUL2.1 QA5 QV2 RA5.3 "
    "MUL3.0 MUL3.1 QA8 QV3 QA7 QA3 QA6 QA9 EO8 "
)


def parse(step):
    kind = "".join([ch for ch in step if ch not in "0123456789."])
    return kind, tuple(int(v) for v in step.replace(kind, "").split("."))


def x_set_of(slot):
    return [first for first, slots in X_SETS.items() if slot in slots][0]


def a_set_of(block, group):
    return [i for i, tiles in enumerate(A_SETS) if (block, group) in tiles][0]


def inputs_of(kind, at):
    if kind in ("EX", "EP", "EXP", "RA"):
        return [(writer, at) for writer, reader in READER.items() if reader == kind]
    if kind == "EO":
        return [("O", (at[0], GROUPS - 1))]
    if kind == "QX":
        return [("EX", (s,)) for s in X_SETS[at[0]]]
    if kind == "H":
        return [("QX", (x_set_of(at[0]),))]
    if kind == "MUL":
        return [("EXP", (PACK * at[0] + t,)) for t in range(PACK)]
    if kind == "QV":
        return [("MUL", (at[0], h)) for h in range(2)]
    if kind == "QC":
        return [("IC", at)]
    if kind == "QP":
        return [("EP", at)]
    if kind == "A":
        return [("QP", (at[0] // 2,)), ("QC", (at[1],))]
    if kind == "QA":
        return [("RA", tile) for tile in A_SETS[at[0]]]
    if kind == "O":
        return [("QA", (a_set_of(PIECES[at[0]][0], at[1]),)), ("QV", (at[1],))]
    return []


def program():
    tensor_steps = [parse(step) for step in TENSOR_ORDER.split()]
    vector_steps = [parse(step) for step in VECTOR_ORDER.split()]
    readers = []
    for kind, at in tensor_steps:
        if kind in READER:
            readers.append((READER[kind], at))
        elif at[1] == GROUPS - 1:
            readers.append(("EO", at[:1]))
    scalar_steps = [step for step in readers if step not in vector_steps]

    queues = [scalar_steps, vector_steps, tensor_steps]
    written, text, free_banks = set(), [], BANKS
    for count in range(sum(len(queue) for queue in queues)):
        ready = []
        for queue in queues:
            if queue and all(step in written for step in inputs_of(*queue[0])):
                kind, at = queue[0]
                opens_bank = kind in READER or (kind == "O" and at[1] == 0)
                if free_banks > 0 or not opens_bank:
                    ready.append((queue, opens_bank))
        queue, opens_bank = ready[0]
        step = queue[0]
        queue.remove(step)
        written.add(step)
        text.append((step[0], step[1], queue is scalar_steps))
        free_banks += (1 if step in readers else 0) - (1 if opens_bank else 0)
    return text


def tile_cox_risk_sums_s11_kernel(tc, x, b_words, b_scales, z, phi, c, out):
    nc = tc.nc
    with ExitStack() as ctx:
        keep = ctx.enter_context(tc.tile_pool(name="keep", bufs=1))
        stage = ctx.enter_context(tc.tile_pool(name="stage", bufs=2))
        psum = ctx.enter_context(tc.psum_pool(name="psum", bufs=1))
        ctx.enter_context(tc.manual_schedule())

        def quantise(name, src):
            words = src.shape[1] // PACK
            codes = keep.tile([P, words], U32, name=name + "_codes", align_bytes=64)
            scales = keep.tile([P, words], U8, name=name + "_scales", align_bytes=64)
            nc.vector.quantize_mx(out=codes[:].bitcast(FP8X4), scales=scales[:], in_=src)
            return codes, scales

        def mx_pass(dst, lhs, lhs_cols, rhs, rhs_cols, start, stop):
            nc.tensor.matmul_mx(out=dst, lhsT=lhs[0][:, lhs_cols].bitcast(FP8X4), lhsT_scale=lhs[1][:, lhs_cols],
                                rhs=rhs[0][:, rhs_cols].bitcast(FP8X4), rhs_scale=rhs[1][:, rhs_cols],
                                start=start, stop=stop)

        def columns(index, width):
            return slice(index * width, (index + 1) * width)

        ident = keep.tile([P, P], F32, name="ident")
        make_identity(nc, ident[:])
        table_probe = keep.tile([P, 8], F32, name="table_probe")
        b_scale_plane = keep.tile([P, 2 * MODELS], U8, name="b_scale_plane", align_bytes=64)
        ones = keep.tile([P, PACK * P], BF16, name="ones", align_bytes=64)
        nc.vector.memset(ones[:].bitcast(I32), BF16_ONE_PAIR)
        nc.vector.memset(table_probe[:, 0:4], 0.0)
        ones_mx = quantise("ones", ones[:])
        nc.vector.memset(b_scale_plane[:].bitcast(I32), 0)
        nc.scalar.activation(out=table_probe[:, 4:5], in_=table_probe[:, 0:1], func=ACT.Exp)
        b_codes = keep.tile([P, 2 * 2 * MODELS], U8, name="b_codes", align_bytes=64)

        x_rows = x.rearrange("(g m t) k -> g m (t k)", g=GROUPS, t=PACK)
        z_rows = z.rearrange("(g m t) r -> g m (t r)", g=GROUPS, t=PACK)
        c_rows = c.rearrange("(p j) n -> p j n", j=PACK)
        phi_rows = phi.rearrange("(p b) j -> p (b j)", b=BLOCKS)
        out_rows = out.rearrange("(p b) r -> p b r", b=BLOCKS)

        x_tiles = [keep.tile([P, 2 * COVARIATES], BF16, name="x%d" % i, align_bytes=64) for i in range(8)]
        phi_tiles = [keep.tile([P, 2 * BASIS], BF16, name="phi%d" % i, align_bytes=64) for i in range(BLOCKS // 2)]
        z_tiles = [keep.tile([P, PACK * MODELS], BF16, name="z%d" % g, align_bytes=64) for g in range(GROUPS)]
        cv_tiles = [keep.tile([P, PACK * BANK], BF16, name="cv%d" % g, align_bytes=64) for g in range(GROUPS)]
        a_tiles = [keep.tile([P, len(tiles) * BANK], BF16, name="a%d" % i, align_bytes=64)
                   for i, tiles in enumerate(A_SETS)]

        for load in LOAD_ORDER.split():
            if load == "bw":
                nc.sync.dma_start(out=b_codes[:].bitcast(I32).rearrange("p (h n) -> p h n", h=2),
                                  in_=b_words.bitcast(I32).rearrange("h p n -> p h n"))
            elif load == "bs":
                for q in range(4):
                    nc.sync.dma_start(
                        out=b_scale_plane[32 * q:32 * q + 4, :].bitcast(I32).rearrange("r (h n) -> r h n", h=2),
                        in_=b_scales.bitcast(I32)[:, 4 * q:4 * q + 4, :].rearrange("h r n -> r h n"))
            else:
                kind, (i,) = parse(load)
                if kind == "x":
                    width = COVARIATES * (1 if i < X_SINGLE_LOADS else 2)
                    g, t = divmod(i, PACK)
                    nc.sync.dma_start(out=x_tiles[i // 2][:, (i % 2) * COVARIATES:(i % 2) * COVARIATES + width],
                                      in_=x_rows[g, :, t * COVARIATES:t * COVARIATES + width])
                elif kind == "z":
                    nc.sync.dma_start(out=z_tiles[i][:], in_=z_rows[i])
                elif kind == "c":
                    nc.sync.dma_start(out=cv_tiles[i][:].rearrange("p (j n) -> p j n", j=PACK),
                                      in_=c_rows[:, :, columns(i, BANK)])
                else:
                    nc.sync.dma_start(out=phi_tiles[i][:], in_=phi_rows[:, columns(i, 2 * BASIS)])

        free_banks = list(range(BANKS))
        bank_of, bank_index = {}, {}

        def new_bank(index):
            return psum.tile([P, BANK], F32, name="bank%d" % index, tag="bank%d" % index)

        def open_bank(key):
            bank_index[key] = free_banks[0]
            free_banks.remove(bank_index[key])
            bank_of[key] = new_bank(bank_index[key])
            return bank_of[key]

        def close_bank(key):
            free_banks.append(bank_index[key])
            return bank_of[key]

        def copy(on_scalar, dst, src):
            if on_scalar:
                nc.scalar.copy(out=dst, in_=src)
            else:
                nc.vector.tensor_copy(out=dst, in_=src)

        def transpose_words(key, words):
            bank = open_bank(key)
            for h in range(2):
                for u in range(2):
                    nc.tensor.transpose(bank[:, columns(2 * h + u, P)], words[:, 2 * P * h + u:2 * P * (h + 1):2],
                                        ident[:])

        def copy_words_out(key, words, on_scalar):
            copy(on_scalar, words.rearrange("q (h m u) -> q h m u", h=2, u=2),
                 close_bank(key)[:].rearrange("q (h u m) -> q h m u", h=2, u=2))

        def x_words(slot):
            return x_tiles[slot // 2][:].bitcast(F32)[:, columns(slot % 2, BANK)]

        warm_bank = new_bank(BANKS - 1)
        for i in range(WARM_PASSES):
            mx_pass(warm_bank[:, columns(i % PACK, P)], ones_mx, columns(0, P), ones_mx, columns(0, P), True, True)

        x_mx, phi_mx, c_mx, v_mx, a_mx, hazard, c_grouped = {}, {}, {}, {}, {}, {}, {}
        for kind, at, on_scalar in program():
            if kind == "TX":
                transpose_words(("X", at), x_words(at[0]))
            elif kind == "EX":
                copy_words_out(("X", at), x_words(at[0]), on_scalar)
            elif kind == "QX":
                first = (at[0] % 2) * COVARIATES
                x_mx[at[0]] = quantise("xq%d" % at,
                                       x_tiles[at[0] // 2][:, first:first + len(X_SETS[at[0]]) * COVARIATES])
            elif kind == "H":
                first = x_set_of(at[0])
                codes, scales = x_mx[first]
                bank = open_bank(("H", at))
                for h in range(2):
                    cols = columns(2 * (at[0] - first) + h, P)
                    nc.tensor.matmul_mx(out=bank[:], lhsT=codes[:, cols].bitcast(FP8X4), lhsT_scale=scales[:, cols],
                                        rhs=b_codes[:, columns(h, 2 * MODELS)].bitcast(FP4X4),
                                        rhs_scale=b_scale_plane[:, columns(h, MODELS)], start=(h == 0), stop=(h == 1))
            elif kind == "EXP":
                g, t = divmod(at[0], PACK)
                if g not in hazard:
                    hazard[g] = stage.tile([P, PACK * MODELS], F32, name="hazard", tag="hazard", bufs=GROUPS,
                                           align_bytes=64)
                nc.scalar.activation(out=hazard[g][:, columns(t, MODELS)], in_=close_bank(("H", at))[:], func=ACT.Exp)
            elif kind == "MUL":
                g, half = at[0], columns(at[1], MODELS // (2 * 4))
                nc.vector.tensor_tensor(
                    out=cv_tiles[g][:].rearrange("p (c i t) -> p c t i", i=4, t=PACK)[:, half],
                    in0=hazard[g][:].rearrange("p (t c i) -> p c t i", i=4, t=PACK)[:, half],
                    in1=z_tiles[g][:].rearrange("p (t c i) -> p c t i", i=4, t=PACK)[:, half],
                    op=mybir.AluOpType.mult)
            elif kind == "QV":
                v_mx[at[0]] = quantise("vq%d" % at, cv_tiles[at[0]][:])
            elif kind == "IC":
                c_grouped[at[0]] = stage.tile([P, PACK * BANK], BF16, name="c_grouped", tag="c_grouped",
                                              align_bytes=64)
                nc.vector.tensor_copy(
                    out=c_grouped[at[0]][:].rearrange("p (t a d j) -> p a t d j", t=PACK, d=2, j=PACK),
                    in_=cv_tiles[at[0]][:].rearrange("p (j a d t) -> p a t d j", j=PACK, d=2, t=PACK))
            elif kind == "QC":
                c_mx[at[0]] = quantise("cq%d" % at, c_grouped[at[0]][:])
            elif kind == "TP":
                transpose_words(("P", at), phi_tiles[at[0]][:].bitcast(F32))
            elif kind == "EP":
                copy_words_out(("P", at), phi_tiles[at[0]][:].bitcast(F32), on_scalar)
            elif kind == "QP":
                phi_mx[at[0]] = quantise("pq%d" % at, phi_tiles[at[0]][:])
            elif kind == "A":
                b, g = at
                bank = open_bank(("A", at))
                for t in range(PACK):
                    mx_pass(bank[:, columns(t, P)], c_mx[g], columns(t, P), phi_mx[b // 2], columns(b % 2, P),
                            True, True)
            elif kind == "RA":
                a_set = a_set_of(*at)
                dst = a_tiles[a_set][:, columns(A_SETS[a_set].index(at), BANK)]
                dst = dst.rearrange("m (c i t) -> m c t i", i=2, t=PACK)
                src = close_bank(("A", at))[:].rearrange("m (t c i) -> m c t i", i=2, t=PACK)
                if on_scalar:
                    nc.scalar.activation(out=dst, in_=src, func=ACT.Relu)
                else:
                    nc.vector.tensor_scalar_max(out=dst, in0=src, scalar1=0.0)
            elif kind == "QA":
                a_mx[at[0]] = quantise("aq%d" % at, a_tiles[at[0]][:])
            elif kind == "O":
                piece, g = at
                b, first, width = PIECES[piece]
                if g == 0:
                    open_bank(("O", piece))
                a_set = a_set_of(b, g)
                mx_pass(bank_of[("O", piece)][:, 0:width], a_mx[a_set], columns(A_SETS[a_set].index((b, g)), P),
                        v_mx[g], slice(first, first + width), g == 0, g == GROUPS - 1)
            else:
                b, first, width = PIECES[at[0]]
                result = stage.tile([P, width], F32, name="result", tag="result", bufs=BLOCKS)
                copy(on_scalar, result[:], close_bank(("O", at[0]))[:, 0:width])
                nc.sync.dma_start(out=out_rows[:, b, first:first + width], in_=result[:])
